import numpy as np
import ml_dtypes


def mxq(x, axis, fmt="e4m3"):
    dtype, down = {"e4m3": (ml_dtypes.float8_e4m3fn, 7), "e5m2": (ml_dtypes.float8_e5m2, 14)}[fmt]
    v = np.moveaxis(np.asarray(x, np.float32).astype(ml_dtypes.bfloat16).astype(np.float64), axis, -1)
    blocks = v.reshape(v.shape[:-1] + (-1, 32))
    amax = np.abs(blocks).max(-1, keepdims=True)
    byte = np.maximum(np.where(amax > 0, np.frexp(amax)[1] - 1 + 127, 0) - down, 1)
    scale = np.exp2(byte - 127.0)
    codes = (blocks / scale).astype(np.float32).astype(dtype).astype(np.float64)
    return np.moveaxis((codes * scale).reshape(v.shape), -1, axis)


WIDE = False


def mx_kscale(k):
    if not WIDE:
        return np.ones(k)
    levels = np.array([30, -30])
    if k % 512:
        return np.exp2(np.random.permutation(np.resize(levels, k // 32))).repeat(32)
    a = np.empty((k // 512, 16))
    for p in range(k // 512):
        a[p, :8] = np.random.permutation(np.resize(levels, 8))
        for g in range(8):
            far = levels[np.abs(levels - a[p, g]) >= 10]
            a[p, g + 8] = far[np.random.randint(len(far))]
    return np.exp2(a.ravel()).repeat(32)


def f64(x):
    return np.asarray(x).astype(np.float64)


def striped(idx):
    return np.tile(np.asarray(idx).reshape(-1, 16).T, (8, 1)).astype(np.uint16)


def unstriped(offs):
    return offs[:16].T.reshape(-1).astype(np.int64)


E2M1 = np.array([0.0, 0.5, 1.0, 1.5, 2.0, 3.0, 4.0, 6.0, -0.0, -0.5, -1.0, -1.5, -2.0, -3.0, -4.0, -6.0])


def pack_weight(w, fmt):
    k, n = w.shape
    w = f64(np.asarray(w, np.float32).astype(ml_dtypes.bfloat16)).reshape(k // 32, 32, n)
    amax = np.abs(w).max(1)
    if fmt == "e4m3":
        byte = np.frexp(amax)[1] - 1 + 127 - 7
    else:
        mant, ex = np.frexp(amax / 6.0)
        byte = np.where(mant > 0.5, ex, ex - 1) + 127
    byte = np.clip(np.where(amax > 0, byte, 1), 1, 254)
    scaled = (w * np.exp2(127.0 - byte)[:, None, :]).reshape(k, n).astype(np.float32)
    by_word = np.ascontiguousarray(scaled.reshape(k // 512, 128, 4, n).transpose(0, 1, 3, 2))
    if fmt == "e4m3":
        words = by_word.astype(ml_dtypes.float8_e4m3fn).view(np.uint8)
    else:
        c = by_word.astype(ml_dtypes.float4_e2m1fn).view(np.uint8) & 0xF
        words = (c[..., 0::2] | (c[..., 1::2] << 4)).reshape(k // 512, 128, 2 * n)
    return np.ascontiguousarray(words), np.ascontiguousarray(byte.astype(np.uint8).reshape(k // 512, 16, n))


def unpack_weight(words, scales, fmt):
    g, _, n = scales.shape
    words = np.ascontiguousarray(words).reshape(g, 128, n, -1)
    if fmt == "e4m3":
        vals = words.view(ml_dtypes.float8_e4m3fn).astype(np.float64)
    else:
        nib = np.empty((g, 128, n, 4), np.uint8)
        nib[..., 0::2] = words & 0xF
        nib[..., 1::2] = words >> 4
        vals = E2M1[nib]
    vals = vals * np.repeat(np.exp2(scales.astype(np.float64) - 127.0), 8, axis=1)[..., None]
    return vals.transpose(0, 1, 3, 2).reshape(g * 512, n)


K, T, J, R, F, Z, C, O, N, S = 512, 1024, 256, 512, 512, 1024, 512, 128, 256, 1024


def setup_inputs():
    n = np.random.standard_normal
    idx = np.random.permutation(T)[:J]
    idx2 = np.random.permutation(Z)[:J]
    idx3 = np.random.permutation(C)[:J]
    idx4 = np.random.permutation(C)[:C]
    idx5 = np.random.permutation(C)[:O]
    idx6 = np.random.permutation(J)[:O]
    idx7 = np.random.permutation(S)[:N]
    ff = mx_kscale(F)
    fk = mx_kscale(K)
    fr = mx_kscale(R)
    xop = pack_weight(n((F, Z)) / ff[:, None], "e4m3")
    wp = pack_weight(n((K, R)) * 1 / np.sqrt(K) / fk[:, None] * fr, "e4m3")
    w2p = pack_weight(n((F, R)) * 1 / np.sqrt(F) * ff[:, None], "e2m1")
    vsp = pack_weight(n((R, S)) * 1 / np.sqrt(R) / fr[:, None], "e2m1")
    return {
        "xo_words": xop[0],
        "xo_scales": xop[1],
        "cq": (np.random.randint(-7, 8, (K, T)).astype(np.float64)).astype(np.float32),
        "gs": (np.random.uniform(0.1, 0.4, (K, 1)) * fk[:, None]).astype(np.float32),
        "w_words": wp[0],
        "w_scales": wp[1],
        "w2_words": w2p[0],
        "w2_scales": w2p[1],
        "vs_words": vsp[0],
        "vs_scales": vsp[1],
        "offs": striped(idx),
        "offs2": striped(idx2),
        "offs3": striped(idx3),
        "offs4": striped(idx4),
        "offs5": striped(idx5),
        "offs6": striped(idx6),
        "offs7": striped(idx7),
    }


def reference(xo_words, xo_scales, cq, gs, w_words, w_scales, w2_words, w2_scales, vs_words, vs_scales, offs, offs2, offs3, offs4, offs5, offs6, offs7):
    idx = unstriped(offs)
    idx2 = unstriped(offs2)
    idx3 = unstriped(offs3)
    idx4 = unstriped(offs4)
    idx5 = unstriped(offs5)
    idx6 = unstriped(offs6)
    idx7 = unstriped(offs7)
    xou = unpack_weight(xo_words, xo_scales, "e4m3")
    wu = unpack_weight(w_words, w_scales, "e4m3")
    w2u = unpack_weight(w2_words, w2_scales, "e2m1")
    vsu = unpack_weight(vs_words, vs_scales, "e2m1")
    x1 = f64(cq)[:, idx] * f64(gs)
    x1q = mxq(x1, 0, "e4m3")
    a = wu.T @ x1q
    xoidx2g = xou[:, idx2]
    b = w2u.T @ xoidx2g
    lb = b[:, 0:1]
    la = a[:, 0:1]
    pw = np.zeros((R, C))
    pw[:, idx3] = a
    pg = np.maximum(pw, pw[:, idx4] * lb)
    hid = np.abs(pg[:, idx5] - b[:, idx6] * la)
    vsidx7g = vsu[:, idx7]
    hidq = mxq(hid, 0, "e5m2")
    y = vsidx7g.T @ hidq
    return y

@@ -1,0 +1,208 @@
+from contextlib import ExitStack
+
+import concourse.mybir as mybir
+
+K, T, J, R, F, Z, C, O, N, S = 512, 1024, 256, 512, 512, 1024, 512, 128, 256, 1024
+FLOPS = 2 * K * R * J + 2 * F * R * J + 2 * R * N * O
+
+F32 = mybir.dt.float32
+BF16 = mybir.dt.bfloat16
+I32 = mybir.dt.int32
+U32 = mybir.dt.uint32
+U16 = mybir.dt.uint16
+U8 = mybir.dt.uint8
+E4M3X4 = mybir.dt.float8_e4m3fn_x4
+E5M2X4 = mybir.dt.float8_e5m2_x4
+E2M1X4 = mybir.dt.float4_e2m1fn_x4
+COPY = mybir.ActivationFunctionType.Copy
+ABS = mybir.ActivationFunctionType.Abs
+ALU = mybir.AluOpType
+
+P = 128
+PACK = 4
+QUADS = 4
+BOARD = 1024
+
+
+def tile_list_leadladder_codednote_store_plain_kernel(
+    tc, xo_words, xo_scales, cq, gs, w_words, w_scales, w2_words, w2_scales, vs_words, vs_scales,
+    offs, offs2, offs3, offs4, offs5, offs6, offs7, out,
+):
+    nc = tc.nc
+    with ExitStack() as ctx:
+        keep = ctx.enter_context(tc.tile_pool(name="keep", bufs=1))
+        reuse = ctx.enter_context(tc.tile_pool(name="reuse", bufs=1))
+        psum = ctx.enter_context(tc.psum_pool(name="psum", bufs=1))
+
+        def sb(name, shape, dtype, tag=None):
+            return keep.tile(shape, dtype, name=name, tag=tag or name, align_bytes=64)
+
+        def placed(name, shape, dtype, offset):
+            return reuse.tile(shape, dtype, name=name, align_bytes=64, offset=offset)
+
+        def load_list(name, src):
+            tile = sb(name, list(src.shape), U16)
+            nc.sync.dma_start(tile[:], src)
+            return tile
+
+        def load_scale_rows(dst, scales):
+            nc.sync.dma_start(dst, scales[0].bitcast(I32).rearrange("(q r) c -> r q c", r=PACK))
+
+        def spread_scale_rows(plane, staged):
+            for q in range(QUADS):
+                nc.vector.tensor_copy(plane[32 * q : 32 * q + PACK, :].bitcast(I32), staged[:, q, :])
+
+        xo_plane = sb("xo_plane", [P, Z], U8)
+        ww_plane = sb("ww_plane", [P, 2 * R], U8)
+        for plane in (xo_plane, ww_plane):
+            nc.vector.memset(plane[:].bitcast(I32), 0)
+        pw = [sb("pw%d" % t, [P, BOARD], F32) for t in range(PACK)]
+        for t in range(PACK):
+            nc.vector.memset(pw[t][:, 0:C], 0.0)
+
+        idx2 = load_list("idx2", offs2)
+        xo_staged = sb("xo_staged", [PACK, QUADS, Z // 4], I32)
+        load_scale_rows(xo_staged[:], xo_scales)
+        ww_staged = sb("ww_staged", [PACK, QUADS, 2 * R // 4], I32)
+        load_scale_rows(ww_staged[:, :, 0 : R // 4], w_scales)
+        load_scale_rows(ww_staged[:, :, R // 4 : 2 * R // 4], w2_scales)
+        xo_all = sb("xo_all", [P, Z], U32)
+        nc.sync.dma_start(xo_all[:].bitcast(I32), xo_words[0].rearrange("p c r -> p (c r)").bitcast(I32))
+        w2_raw = sb("w2_raw", [P, R], U16)
+        nc.sync.dma_start(w2_raw[:].bitcast(I32), w2_words[0].bitcast(I32))
+        cq_rows = cq.rearrange("(p t) c -> t p c", t=PACK)
+        cq_sb = [sb("cq%d" % t, [P, T], F32) for t in range(PACK - 1)] + [placed("cq3", [P, T], F32, 0)]
+        for t in range(2):
+            nc.sync.dma_start(cq_sb[t][:], cq_rows[t])
+        idx = load_list("idx", offs)
+        step = sb("step", [P, PACK], F32)
+        nc.sync.dma_start(step[:], gs.rearrange("(p t) o -> p (t o)", t=PACK))
+        nc.sync.dma_start(cq_sb[2][:], cq_rows[2])
+        vs_staged = sb("vs_staged", [PACK, QUADS, S // 4], I32)
+        load_scale_rows(vs_staged[:], vs_scales)
+        idx7 = load_list("idx7", offs7)
+        nc.sync.dma_start(cq_sb[3][:], cq_rows[3])
+        w_raw = placed("w_raw", [P, R], U32, 4096)
+        nc.sync.dma_start(w_raw[:].bitcast(I32), w_words[0].rearrange("p c r -> p (c r)").bitcast(I32))
+        idx3 = load_list("idx3", offs3)
+        vs_all = sb("vs_all", [P, S], U16)
+        nc.sync.dma_start(vs_all[:].bitcast(I32), vs_words[0].bitcast(I32))
+        idx4 = load_list("idx4", offs4)
+        idx6 = load_list("idx6", offs6)
+        idx5 = load_list("idx5", offs5)
+
+        spread_scale_rows(xo_plane, xo_staged)
+        xo_sc = sb("xo_sc", [P, J], U8)
+        nc.vector.tensor_copy(xo_sc[:], xo_plane[:].indirect(idx2[:]))
+        spread_scale_rows(ww_plane, ww_staged)
+        ww_sc = sb("ww_sc", [P, 2 * R], U8)
+        nc.vector.tensor_copy(
+            ww_sc[:].rearrange("p (u t m) -> p u t m", u=2, t=PACK),
+            ww_plane[:].rearrange("p (u m t) -> p u t m", u=2, t=PACK),
+        )
+        xo_g = sb("xo_g", [P, J], U32)
+        nc.vector.tensor_copy(xo_g[:], xo_all[:].indirect(idx2[:]))
+        w2_dealt = sb("w2_dealt", [P, R], U16)
+        nc.scalar.copy(
+            w2_dealt[:].rearrange("p (t m) -> p t m", t=PACK),
+            w2_raw[:].rearrange("p (m t) -> p t m", t=PACK),
+        )
+        b_sb = [placed("b%d" % t, [P, J], F32, 2048 + 1024 * t) for t in range(PACK)]
+        b_acc = []
+        for t in range(PACK):
+            acc = psum.tile([P, J], F32, name="b_acc%d" % t, tag="bank_b%d" % t)
+            b_acc.append(acc)
+            nc.tensor.matmul_mx(
+                acc[:],
+                lhsT=w2_dealt[:, t * P : (t + 1) * P].bitcast(E2M1X4),
+                lhsT_scale=ww_sc[:, R + t * P : R + (t + 1) * P],
+                rhs=xo_g[:].bitcast(E4M3X4),
+                rhs_scale=xo_sc[:],
+                start=True,
+                stop=True,
+            )
+
+        vs_plane = sb("vs_plane", [P, S], U8, tag="xo_all")
+        nc.vector.memset(vs_plane[:].bitcast(I32), 0)
+        spread_scale_rows(vs_plane, vs_staged)
+        vs_sc = sb("vs_sc", [P, N], U8)
+        nc.vector.tensor_copy(vs_sc[:], vs_plane[:].indirect(idx7[:]))
+
+        x1_planes = sb("x1_planes", [P, PACK, J], BF16)
+        for t in range(PACK):
+            nc.scalar.activation(x1_planes[:, t, :], cq_sb[t][:].indirect(idx[:]), COPY, scale=step[:, t : t + 1])
+        w_dealt = placed("w_dealt", [P, R], U32, 0)
+        nc.scalar.copy(
+            w_dealt[:].rearrange("p (t m) -> p t m", t=PACK),
+            w_raw[:].rearrange("p (m t) -> p t m", t=PACK),
+        )
+        for t in range(PACK):
+            nc.scalar.copy(b_sb[t][:], b_acc[t][:])
+        x1_woven = sb("x1_woven", [P, J, PACK], BF16)
+        nc.vector.tensor_copy(
+            x1_woven[:].rearrange("p (c i) t -> p c t i", i=4),
+            x1_planes[:].rearrange("p t (c i) -> p c t i", i=4),
+        )
+        x1_codes = sb("x1_codes", [P, J], U32)
+        x1_sc = sb("x1_sc", [P, J], U8)
+        nc.vector.quantize_mx(x1_codes[:].bitcast(E4M3X4), x1_sc[:], x1_woven[:].rearrange("p j t -> p (j t)"))
+
+        vs_g = sb("vs_g", [P, N], U16, tag="x1_woven")
+        nc.vector.tensor_copy(vs_g[:], vs_all[:].indirect(idx7[:]))
+
+        a_sb = [sb("a%d" % t, [P, J], F32) for t in range(PACK)]
+        for t in range(PACK):
+            acc = psum.tile([P, J], F32, name="a_acc%d" % t, tag="bank_a%d" % t)
+            nc.tensor.matmul_mx(
+                acc[:],
+                lhsT=w_dealt[:, t * P : (t + 1) * P].bitcast(E4M3X4),
+                lhsT_scale=ww_sc[:, t * P : (t + 1) * P],
+                rhs=x1_codes[:].bitcast(E4M3X4),
+                rhs_scale=x1_sc[:],
+                start=True,
+                stop=True,
+            )
+            if t == 0:
+                nc.vector.tensor_copy(a_sb[t][:], acc[:])
+            else:
+                nc.scalar.copy(a_sb[t][:], acc[:])
+
+        nc.vector.tensor_copy(pw[0][:].indirect(idx3[:]), a_sb[0][:])
+        nc.scalar.activation(pw[1][:].indirect(idx3[:]), a_sb[1][:], COPY)
+        nc.vector.tensor_copy(pw[2][:].indirect(idx3[:]), a_sb[2][:])
+        nc.vector.tensor_copy(pw[3][:].indirect(idx3[:]), a_sb[3][:])
+
+        diff = sb("diff", [P, PACK, O], F32)
+        for t in range(PACK):
+            rival = sb("rival%d" % t, [P, C], F32)
+            nc.scalar.activation(rival[:], pw[t][:].indirect(idx4[:]), COPY, scale=b_sb[t][:, 0:1])
+            b_led = sb("b_led%d" % t, [P, O], F32)
+            nc.scalar.activation(b_led[:], b_sb[t][:].indirect(idx6[:]), COPY, scale=a_sb[t][:, 0:1])
+            pg = sb("pg%d" % t, [P, C], F32)
+            nc.vector.tensor_tensor(pg[:], pw[t][:, 0:C], rival[:], ALU.max)
+            nc.vector.tensor_tensor(diff[:, t, :], pg[:].indirect(idx5[:]), b_led[:], ALU.subtract)
+
+        hid = sb("hid", [P, O, PACK], BF16)
+        nc.scalar.activation(hid[:], diff[:].rearrange("p t o -> p o t"), ABS)
+        hid_codes = sb("hid_codes", [P, O], U32)
+        hid_sc = sb("hid_sc", [P, O], U8)
+        nc.vector.quantize_mx(hid_codes[:].bitcast(E5M2X4), hid_sc[:], hid[:].rearrange("p o t -> p (o t)"))
+
+        for h in range(N // P):
+            acc = psum.tile([P, O], F32, name="y_acc%d" % h, tag="bank_b%d" % h)
+            nc.tensor.matmul_mx(
+                acc[:],
+                lhsT=vs_g[:, h * P : (h + 1) * P].bitcast(E2M1X4),
+                lhsT_scale=vs_sc[:, h * P : (h + 1) * P],
+                rhs=hid_codes[:].bitcast(E5M2X4),
+                rhs_scale=hid_sc[:],
+                start=True,
+                stop=True,
+            )
+            y = sb("y%d" % h, [P, O], F32)
+            if h == 0:
+                nc.vector.tensor_copy(y[:], acc[:])
+                nc.sync.dma_start(out[0:P, :], y[:])
+            else:
+                nc.scalar.copy(y[:], acc[:])
+                nc.scalar.dma_start(out[P : 2 * P, :], y[:])

@@ -34,8 +34,8 @@ def tile_list_leadladder_codednote_store_plain_kernel(
         reuse = ctx.enter_context(tc.tile_pool(name="reuse", bufs=1))
         psum = ctx.enter_context(tc.psum_pool(name="psum", bufs=1))
 
-        def sb(name, shape, dtype, tag=None):
-            return keep.tile(shape, dtype, name=name, tag=tag or name, align_bytes=64)
+        def sb(name, shape, dtype):
+            return keep.tile(shape, dtype, name=name, align_bytes=64)
 
         def placed(name, shape, dtype, offset):
             return reuse.tile(shape, dtype, name=name, align_bytes=64, offset=offset)
@@ -45,86 +45,66 @@ def tile_list_leadladder_codednote_store_plain_kernel(
             nc.sync.dma_start(tile[:], src)
             return tile
 
-        def load_scale_rows(dst, scales):
-            nc.sync.dma_start(dst, scales[0].bitcast(I32).rearrange("(q r) c -> r q c", r=PACK))
+        def load_scale_rows(staged, row0, scales):
+            nc.sync.dma_start(
+                staged[row0 : row0 + PACK, :, :], scales[0].bitcast(I32).rearrange("(q r) c -> r q c", r=PACK)
+            )
 
-        def spread_scale_rows(plane, staged):
+        def spread_scale_rows(plane, staged, row0, rows):
             for q in range(QUADS):
-                nc.vector.tensor_copy(plane[32 * q : 32 * q + PACK, :].bitcast(I32), staged[:, q, :])
+                nc.vector.tensor_copy(plane[32 * q : 32 * q + rows, :].bitcast(I32), staged[row0 : row0 + rows, q, :])
 
+        def deal(copy, dst, src):
+            copy(dst[:].rearrange("p (t m) -> p m t", t=PACK), src[:].rearrange("p (m t) -> p m t", t=PACK))
+
+        ww_staged = sb("ww_staged", [P, QUADS, R // 4], I32)
+        nc.vector.memset(ww_staged[64:96, :, :], 0)
+        vs_staged = sb("vs_staged", [P, QUADS, S // 4], I32)
+        nc.vector.memset(vs_staged[96:128, :, :], 0)
         xo_plane = sb("xo_plane", [P, Z], U8)
-        ww_plane = sb("ww_plane", [P, 2 * R], U8)
-        for plane in (xo_plane, ww_plane):
-            nc.vector.memset(plane[:].bitcast(I32), 0)
+        nc.vector.memset(xo_plane[:].bitcast(I32), 0)
         pw = [sb("pw%d" % t, [P, BOARD], F32) for t in range(PACK)]
         for t in range(PACK):
             nc.vector.memset(pw[t][:, 0:C], 0.0)
 
-        idx2 = load_list("idx2", offs2)
         xo_staged = sb("xo_staged", [PACK, QUADS, Z // 4], I32)
-        load_scale_rows(xo_staged[:], xo_scales)
-        ww_staged = sb("ww_staged", [PACK, QUADS, 2 * R // 4], I32)
-        load_scale_rows(ww_staged[:, :, 0 : R // 4], w_scales)
-        load_scale_rows(ww_staged[:, :, R // 4 : 2 * R // 4], w2_scales)
-        xo_all = sb("xo_all", [P, Z], U32)
-        nc.sync.dma_start(xo_all[:].bitcast(I32), xo_words[0].rearrange("p c r -> p (c r)").bitcast(I32))
-        w2_raw = sb("w2_raw", [P, R], U16)
-        nc.sync.dma_start(w2_raw[:].bitcast(I32), w2_words[0].bitcast(I32))
-        cq_rows = cq.rearrange("(p t) c -> t p c", t=PACK)
-        cq_sb = [sb("cq%d" % t, [P, T], F32) for t in range(PACK - 1)] + [placed("cq3", [P, T], F32, 0)]
-        for t in range(2):
-            nc.sync.dma_start(cq_sb[t][:], cq_rows[t])
-        idx = load_list("idx", offs)
+        load_scale_rows(xo_staged, 0, xo_scales)
         step = sb("step", [P, PACK], F32)
         nc.sync.dma_start(step[:], gs.rearrange("(p t) o -> p (t o)", t=PACK))
+        idx = load_list("idx", offs)
+        cq_rows = cq.rearrange("(p t) c -> t p c", t=PACK)
+        cq_sb = [sb("cq%d" % t, [P, T], F32) for t in range(PACK - 1)] + [placed("cq3", [P, T], F32, 0)]
+        nc.sync.dma_start(cq_sb[0][:], cq_rows[0])
+        load_scale_rows(ww_staged, 68, w_scales)
+        load_scale_rows(ww_staged, 64, w2_scales)
+        nc.sync.dma_start(cq_sb[1][:], cq_rows[1])
+        load_scale_rows(vs_staged, 96, vs_scales)
         nc.sync.dma_start(cq_sb[2][:], cq_rows[2])
-        vs_staged = sb("vs_staged", [PACK, QUADS, S // 4], I32)
-        load_scale_rows(vs_staged[:], vs_scales)
+        idx2 = load_list("idx2", offs2)
         idx7 = load_list("idx7", offs7)
         nc.sync.dma_start(cq_sb[3][:], cq_rows[3])
         w_raw = placed("w_raw", [P, R], U32, 4096)
         nc.sync.dma_start(w_raw[:].bitcast(I32), w_words[0].rearrange("p c r -> p (c r)").bitcast(I32))
+        w2_raw = sb("w2_raw", [P, R], U16)
+        nc.sync.dma_start(w2_raw[:].bitcast(I32), w2_words[0].bitcast(I32))
+        xo_all = sb("xo_all", [P, Z], U32)
+        nc.sync.dma_start(xo_all[:].bitcast(I32), xo_words[0].rearrange("p c r -> p (c r)").bitcast(I32))
         idx3 = load_list("idx3", offs3)
-        vs_all = sb("vs_all", [P, S], U16)
-        nc.sync.dma_start(vs_all[:].bitcast(I32), vs_words[0].bitcast(I32))
         idx4 = load_list("idx4", offs4)
         idx6 = load_list("idx6", offs6)
         idx5 = load_list("idx5", offs5)
+        vs_all = sb("vs_all", [P, S], U16)
+        nc.sync.dma_start(vs_all[:].bitcast(I32), vs_words[0].bitcast(I32))
 
-        spread_scale_rows(xo_plane, xo_staged)
+        spread_scale_rows(xo_plane, xo_staged, 0, PACK)
+        ww_plane = sb("ww_plane", [P, R], U8)
+        spread_scale_rows(ww_plane, ww_staged, 64, 32)
+        vs_plane = sb("vs_plane", [P, S], U8)
+        spread_scale_rows(vs_plane, vs_staged, 96, 32)
+        ww_sc = sb("ww_sc", [P, R], U8)
+        deal(nc.vector.tensor_copy, ww_sc, ww_plane)
         xo_sc = sb("xo_sc", [P, J], U8)
         nc.vector.tensor_copy(xo_sc[:], xo_plane[:].indirect(idx2[:]))
-        spread_scale_rows(ww_plane, ww_staged)
-        ww_sc = sb("ww_sc", [P, 2 * R], U8)
-        nc.vector.tensor_copy(
-            ww_sc[:].rearrange("p (u t m) -> p u t m", u=2, t=PACK),
-            ww_plane[:].rearrange("p (u m t) -> p u t m", u=2, t=PACK),
-        )
-        xo_g = sb("xo_g", [P, J], U32)
-        nc.vector.tensor_copy(xo_g[:], xo_all[:].indirect(idx2[:]))
-        w2_dealt = sb("w2_dealt", [P, R], U16)
-        nc.scalar.copy(
-            w2_dealt[:].rearrange("p (t m) -> p t m", t=PACK),
-            w2_raw[:].rearrange("p (m t) -> p t m", t=PACK),
-        )
-        b_sb = [placed("b%d" % t, [P, J], F32, 2048 + 1024 * t) for t in range(PACK)]
-        b_acc = []
-        for t in range(PACK):
-            acc = psum.tile([P, J], F32, name="b_acc%d" % t, tag="bank_b%d" % t)
-            b_acc.append(acc)
-            nc.tensor.matmul_mx(
-                acc[:],
-                lhsT=w2_dealt[:, t * P : (t + 1) * P].bitcast(E2M1X4),
-                lhsT_scale=ww_sc[:, R + t * P : R + (t + 1) * P],
-                rhs=xo_g[:].bitcast(E4M3X4),
-                rhs_scale=xo_sc[:],
-                start=True,
-                stop=True,
-            )
-
-        vs_plane = sb("vs_plane", [P, S], U8, tag="xo_all")
-        nc.vector.memset(vs_plane[:].bitcast(I32), 0)
-        spread_scale_rows(vs_plane, vs_staged)
         vs_sc = sb("vs_sc", [P, N], U8)
         nc.vector.tensor_copy(vs_sc[:], vs_plane[:].indirect(idx7[:]))
 
@@ -132,13 +112,10 @@ def tile_list_leadladder_codednote_store_plain_kernel(
         for t in range(PACK):
             nc.scalar.activation(x1_planes[:, t, :], cq_sb[t][:].indirect(idx[:]), COPY, scale=step[:, t : t + 1])
         w_dealt = placed("w_dealt", [P, R], U32, 0)
-        nc.scalar.copy(
-            w_dealt[:].rearrange("p (t m) -> p t m", t=PACK),
-            w_raw[:].rearrange("p (m t) -> p t m", t=PACK),
-        )
-        for t in range(PACK):
-            nc.scalar.copy(b_sb[t][:], b_acc[t][:])
-        x1_woven = sb("x1_woven", [P, J, PACK], BF16)
+        deal(nc.scalar.copy, w_dealt, w_raw)
+        w2_dealt = placed("w2_dealt", [P, R], U16, 4096)
+        deal(nc.scalar.copy, w2_dealt, w2_raw)
+        x1_woven = placed("x1_woven", [P, J, PACK], BF16, 8192)
         nc.vector.tensor_copy(
             x1_woven[:].rearrange("p (c i) t -> p c t i", i=4),
             x1_planes[:].rearrange("p t (c i) -> p c t i", i=4),
@@ -146,50 +123,70 @@ def tile_list_leadladder_codednote_store_plain_kernel(
         x1_codes = sb("x1_codes", [P, J], U32)
         x1_sc = sb("x1_sc", [P, J], U8)
         nc.vector.quantize_mx(x1_codes[:].bitcast(E4M3X4), x1_sc[:], x1_woven[:].rearrange("p j t -> p (j t)"))
+        xo_g = placed("xo_g", [P, J], U32, 8192)
+        nc.vector.tensor_copy(xo_g[:], xo_all[:].indirect(idx2[:]))
 
-        vs_g = sb("vs_g", [P, N], U16, tag="x1_woven")
-        nc.vector.tensor_copy(vs_g[:], vs_all[:].indirect(idx7[:]))
-
-        a_sb = [sb("a%d" % t, [P, J], F32) for t in range(PACK)]
+        a_acc = [psum.tile([P, J], F32, name="a_acc%d" % t, tag="bank_a%d" % t) for t in range(PACK)]
         for t in range(PACK):
-            acc = psum.tile([P, J], F32, name="a_acc%d" % t, tag="bank_a%d" % t)
             nc.tensor.matmul_mx(
-                acc[:],
+                a_acc[t][:],
                 lhsT=w_dealt[:, t * P : (t + 1) * P].bitcast(E4M3X4),
-                lhsT_scale=ww_sc[:, t * P : (t + 1) * P],
+                lhsT_scale=ww_sc[4:P, t * P : (t + 1) * P],
                 rhs=x1_codes[:].bitcast(E4M3X4),
                 rhs_scale=x1_sc[:],
                 start=True,
                 stop=True,
             )
-            if t == 0:
-                nc.vector.tensor_copy(a_sb[t][:], acc[:])
-            else:
-                nc.scalar.copy(a_sb[t][:], acc[:])
+        b_acc = [psum.tile([P, J], F32, name="b_acc%d" % t, tag="bank_b%d" % t) for t in range(PACK)]
+        for t in range(PACK):
+            nc.tensor.matmul_mx(
+                b_acc[t][:],
+                lhsT=w2_dealt[:, t * P : (t + 1) * P].bitcast(E2M1X4),
+                lhsT_scale=ww_sc[:, t * P : (t + 1) * P],
+                rhs=xo_g[:].bitcast(E4M3X4),
+                rhs_scale=xo_sc[:],
+                start=True,
+                stop=True,
+            )
 
+        a_sb = [sb("a%d" % t, [P, J], F32) for t in range(PACK)]
+        b_sb = [sb("b%d" % t, [P, J], F32) for t in range(PACK)]
+        for t in range(3):
+            nc.scalar.copy(a_sb[t][:], a_acc[t][:])
         nc.vector.tensor_copy(pw[0][:].indirect(idx3[:]), a_sb[0][:])
+        nc.vector.tensor_copy(a_sb[3][:], a_acc[3][:])
         nc.scalar.activation(pw[1][:].indirect(idx3[:]), a_sb[1][:], COPY)
         nc.vector.tensor_copy(pw[2][:].indirect(idx3[:]), a_sb[2][:])
         nc.vector.tensor_copy(pw[3][:].indirect(idx3[:]), a_sb[3][:])
+        for t in range(2):
+            nc.scalar.copy(b_sb[t][:], b_acc[t][:])
+        for t in range(2, PACK):
+            nc.vector.tensor_copy(b_sb[t][:], b_acc[t][:])
 
         diff = sb("diff", [P, PACK, O], F32)
-        for t in range(PACK):
-            rival = sb("rival%d" % t, [P, C], F32)
-            nc.scalar.activation(rival[:], pw[t][:].indirect(idx4[:]), COPY, scale=b_sb[t][:, 0:1])
-            b_led = sb("b_led%d" % t, [P, O], F32)
-            nc.scalar.activation(b_led[:], b_sb[t][:].indirect(idx6[:]), COPY, scale=a_sb[t][:, 0:1])
-            pg = sb("pg%d" % t, [P, C], F32)
-            nc.vector.tensor_tensor(pg[:], pw[t][:, 0:C], rival[:], ALU.max)
-            nc.vector.tensor_tensor(diff[:, t, :], pg[:].indirect(idx5[:]), b_led[:], ALU.subtract)
+        rival = [sb("rival%d" % t, [P, C], F32) for t in range(PACK)]
+        pg = [sb("pg%d" % t, [P, C], F32) for t in range(PACK)]
+        b_led = [sb("b_led%d" % t, [P, O], F32) for t in range(PACK - 1)] + [placed("b_led3", [P, O], F32, 12288)]
+        for pair in ((0, 1), (2, 3)):
+            for t in pair:
+                nc.scalar.activation(rival[t][:], pw[t][:].indirect(idx4[:]), COPY, scale=b_sb[t][:, 0:1])
+                nc.vector.tensor_tensor(pg[t][:], pw[t][:, 0:C], rival[t][:], ALU.max)
+            for t in pair:
+                nc.scalar.activation(b_led[t][:], b_sb[t][:].indirect(idx6[:]), COPY, scale=a_sb[t][:, 0:1])
+                nc.vector.tensor_tensor(diff[:, t, :], pg[t][:].indirect(idx5[:]), b_led[t][:], ALU.subtract)
 
         hid = sb("hid", [P, O, PACK], BF16)
-        nc.scalar.activation(hid[:], diff[:].rearrange("p t o -> p o t"), ABS)
+        nc.scalar.activation(
+            hid[:].rearrange("p (c i) t -> p c t i", i=4), diff[:].rearrange("p t (c i) -> p c t i", i=4), ABS
+        )
+        vs_g = placed("vs_g", [P, N], U16, 12288)
+        nc.vector.tensor_copy(vs_g[:], vs_all[:].indirect(idx7[:]))
         hid_codes = sb("hid_codes", [P, O], U32)
         hid_sc = sb("hid_sc", [P, O], U8)
         nc.vector.quantize_mx(hid_codes[:].bitcast(E5M2X4), hid_sc[:], hid[:].rearrange("p o t -> p (o t)"))
 
         for h in range(N // P):
-            acc = psum.tile([P, O], F32, name="y_acc%d" % h, tag="bank_b%d" % h)
+            acc = psum.tile([P, O], F32, name="y_acc%d" % h, tag="bank_a%d" % h)
             nc.tensor.matmul_mx(
                 acc[:],
                 lhsT=vs_g[:, h * P : (h + 1) * P].bitcast(E2M1X4),

@@ -50,22 +50,30 @@ def tile_list_leadladder_codednote_store_plain_kernel(
                 staged[row0 : row0 + PACK, :, :], scales[0].bitcast(I32).rearrange("(q r) c -> r q c", r=PACK)
             )
 
-        def spread_scale_rows(plane, staged, row0, rows):
+        def spread_scale_rows(pairs, row0, rows):
             for q in range(QUADS):
-                nc.vector.tensor_copy(plane[32 * q : 32 * q + rows, :].bitcast(I32), staged[row0 : row0 + rows, q, :])
+                for plane, staged in pairs:
+                    nc.vector.tensor_copy(
+                        plane[32 * q : 32 * q + rows, :].bitcast(I32), staged[row0 : row0 + rows, q, :]
+                    )
 
         def deal(copy, dst, src):
             copy(dst[:].rearrange("p (t m) -> p m t", t=PACK), src[:].rearrange("p (m t) -> p m t", t=PACK))
 
         ww_staged = sb("ww_staged", [P, QUADS, R // 4], I32)
         nc.vector.memset(ww_staged[64:96, :, :], 0)
-        vs_staged = sb("vs_staged", [P, QUADS, S // 4], I32)
-        nc.vector.memset(vs_staged[96:128, :, :], 0)
+        vs_plane = sb("vs_plane", [P, S], U8)
+        nc.vector.memset(vs_plane[:].bitcast(I32), 0)
         xo_plane = sb("xo_plane", [P, Z], U8)
         nc.vector.memset(xo_plane[:].bitcast(I32), 0)
         pw = [sb("pw%d" % t, [P, BOARD], F32) for t in range(PACK)]
         for t in range(PACK):
             nc.vector.memset(pw[t][:, 0:C], 0.0)
+
+        def load_vs_scale_quadrant(q):
+            nc.sync.dma_start(
+                vs_plane[32 * q : 32 * q + PACK, :].bitcast(I32), vs_scales[0, PACK * q : PACK * (q + 1), :].bitcast(I32)
+            )
 
         xo_staged = sb("xo_staged", [PACK, QUADS, Z // 4], I32)
         load_scale_rows(xo_staged, 0, xo_scales)
@@ -78,16 +86,18 @@ def tile_list_leadladder_codednote_store_plain_kernel(
         load_scale_rows(ww_staged, 68, w_scales)
         load_scale_rows(ww_staged, 64, w2_scales)
         nc.sync.dma_start(cq_sb[1][:], cq_rows[1])
-        load_scale_rows(vs_staged, 96, vs_scales)
-        nc.sync.dma_start(cq_sb[2][:], cq_rows[2])
         idx2 = load_list("idx2", offs2)
+        nc.sync.dma_start(cq_sb[2][:], cq_rows[2])
         idx7 = load_list("idx7", offs7)
+        for q in range(QUADS - 1):
+            load_vs_scale_quadrant(q)
         nc.sync.dma_start(cq_sb[3][:], cq_rows[3])
+        load_vs_scale_quadrant(QUADS - 1)
         w_raw = placed("w_raw", [P, R], U32, 4096)
         nc.sync.dma_start(w_raw[:].bitcast(I32), w_words[0].rearrange("p c r -> p (c r)").bitcast(I32))
         w2_raw = sb("w2_raw", [P, R], U16)
         nc.sync.dma_start(w2_raw[:].bitcast(I32), w2_words[0].bitcast(I32))
-        xo_all = sb("xo_all", [P, Z], U32)
+        xo_all = placed("xo_all", [P, Z], U32, 16384)
         nc.sync.dma_start(xo_all[:].bitcast(I32), xo_words[0].rearrange("p c r -> p (c r)").bitcast(I32))
         idx3 = load_list("idx3", offs3)
         idx4 = load_list("idx4", offs4)
@@ -96,11 +106,9 @@ def tile_list_leadladder_codednote_store_plain_kernel(
         vs_all = sb("vs_all", [P, S], U16)
         nc.sync.dma_start(vs_all[:].bitcast(I32), vs_words[0].bitcast(I32))
 
-        spread_scale_rows(xo_plane, xo_staged, 0, PACK)
+        spread_scale_rows([(xo_plane, xo_staged)], 0, PACK)
         ww_plane = sb("ww_plane", [P, R], U8)
-        spread_scale_rows(ww_plane, ww_staged, 64, 32)
-        vs_plane = sb("vs_plane", [P, S], U8)
-        spread_scale_rows(vs_plane, vs_staged, 96, 32)
+        spread_scale_rows([(ww_plane, ww_staged)], 64, 32)
         ww_sc = sb("ww_sc", [P, R], U8)
         deal(nc.vector.tensor_copy, ww_sc, ww_plane)
         xo_sc = sb("xo_sc", [P, J], U8)
@@ -116,13 +124,18 @@ def tile_list_leadladder_codednote_store_plain_kernel(
         w2_dealt = placed("w2_dealt", [P, R], U16, 4096)
         deal(nc.scalar.copy, w2_dealt, w2_raw)
         x1_woven = placed("x1_woven", [P, J, PACK], BF16, 8192)
-        nc.vector.tensor_copy(
-            x1_woven[:].rearrange("p (c i) t -> p c t i", i=4),
-            x1_planes[:].rearrange("p t (c i) -> p c t i", i=4),
-        )
+        halves = [slice(0, J // 2), slice(J // 2, J)]
+        for js in halves:
+            nc.vector.tensor_copy(
+                x1_woven[:, js, :].rearrange("p (c i) t -> p c t i", i=4),
+                x1_planes[:, :, js].rearrange("p t (c i) -> p c t i", i=4),
+            )
         x1_codes = sb("x1_codes", [P, J], U32)
         x1_sc = sb("x1_sc", [P, J], U8)
-        nc.vector.quantize_mx(x1_codes[:].bitcast(E4M3X4), x1_sc[:], x1_woven[:].rearrange("p j t -> p (j t)"))
+        for js in halves:
+            nc.vector.quantize_mx(
+                x1_codes[:, js].bitcast(E4M3X4), x1_sc[:, js], x1_woven[:, js, :].rearrange("p j t -> p (j t)")
+            )
         xo_g = placed("xo_g", [P, J], U32, 8192)
         nc.vector.tensor_copy(xo_g[:], xo_all[:].indirect(idx2[:]))
 
@@ -149,7 +162,7 @@ def tile_list_leadladder_codednote_store_plain_kernel(
                 stop=True,
             )
 
-        a_sb = [sb("a%d" % t, [P, J], F32) for t in range(PACK)]
+        a_sb = [sb("a%d" % t, [P, J], F32) for t in range(PACK - 1)] + [placed("a3", [P, J], F32, 16384)]
         b_sb = [sb("b%d" % t, [P, J], F32) for t in range(PACK)]
         for t in range(3):
             nc.scalar.copy(a_sb[t][:], a_acc[t][:])

@@ -60,6 +60,10 @@ def tile_list_leadladder_codednote_store_plain_kernel(
         def deal(copy, dst, src):
             copy(dst[:].rearrange("p (t m) -> p m t", t=PACK), src[:].rearrange("p (m t) -> p m t", t=PACK))
 
+        warm = sb("warm", [P, 16], F32)
+        nc.gpsimd.memset(warm[:, 0:1], 0.0)
+        nc.scalar.activation(warm[:, 8:9], warm[:, 0:1], COPY)
+
         ww_staged = sb("ww_staged", [P, QUADS, R // 4], I32)
         nc.vector.memset(ww_staged[64:96, :, :], 0)
         vs_plane = sb("vs_plane", [P, S], U8)

from contextlib import ExitStack

import concourse.mybir as mybir

K, T, J, R, F, Z, C, O, N, S = 512, 1024, 256, 512, 512, 1024, 512, 128, 256, 1024
FLOPS = 2 * K * R * J + 2 * F * R * J + 2 * R * N * O

F32 = mybir.dt.float32
BF16 = mybir.dt.bfloat16
I32 = mybir.dt.int32
U32 = mybir.dt.uint32
U16 = mybir.dt.uint16
U8 = mybir.dt.uint8
E4M3X4 = mybir.dt.float8_e4m3fn_x4
E5M2X4 = mybir.dt.float8_e5m2_x4
E2M1X4 = mybir.dt.float4_e2m1fn_x4
COPY = mybir.ActivationFunctionType.Copy
ABS = mybir.ActivationFunctionType.Abs
ALU = mybir.AluOpType

P = 128
PACK = 4
QUADS = 4
BOARD = 1024


def tile_list_leadladder_codednote_store_plain_kernel(
    tc, xo_words, xo_scales, cq, gs, w_words, w_scales, w2_words, w2_scales, vs_words, vs_scales,
    offs, offs2, offs3, offs4, offs5, offs6, offs7, out,
):
    nc = tc.nc
    with ExitStack() as ctx:
        keep = ctx.enter_context(tc.tile_pool(name="keep", bufs=1))
        reuse = ctx.enter_context(tc.tile_pool(name="reuse", bufs=1))
        psum = ctx.enter_context(tc.psum_pool(name="psum", bufs=1))

        def sb(name, shape, dtype):
            return keep.tile(shape, dtype, name=name, align_bytes=64)

        def placed(name, shape, dtype, offset):
            return reuse.tile(shape, dtype, name=name, align_bytes=64, offset=offset)

        def load_list(name, src):
            tile = sb(name, list(src.shape), U16)
            nc.sync.dma_start(tile[:], src)
            return tile

        def load_scale_rows(staged, row0, scales):
            nc.sync.dma_start(
                staged[row0 : row0 + PACK, :, :], scales[0].bitcast(I32).rearrange("(q r) c -> r q c", r=PACK)
            )

        def spread_scale_rows(pairs, row0, rows):
            for q in range(QUADS):
                for plane, staged in pairs:
                    nc.vector.tensor_copy(
                        plane[32 * q : 32 * q + rows, :].bitcast(I32), staged[row0 : row0 + rows, q, :]
                    )

        def deal(copy, dst, src):
            copy(dst[:].rearrange("p (t m) -> p m t", t=PACK), src[:].rearrange("p (m t) -> p m t", t=PACK))

        warm = sb("warm", [P, 16], F32)
        nc.gpsimd.memset(warm[:, 0:1], 0.0)
        nc.scalar.activation(warm[:, 8:9], warm[:, 0:1], COPY)

        ww_staged = sb("ww_staged", [P, QUADS, R // 4], I32)
        nc.vector.memset(ww_staged[64:96, :, :], 0)
        vs_plane = sb("vs_plane", [P, S], U8)
        nc.vector.memset(vs_plane[:].bitcast(I32), 0)
        xo_plane = sb("xo_plane", [P, Z], U8)
        nc.vector.memset(xo_plane[:].bitcast(I32), 0)
        pw = [sb("pw%d" % t, [P, BOARD], F32) for t in range(PACK)]
        for t in range(PACK):
            nc.vector.memset(pw[t][:, 0:C], 0.0)

        def load_vs_scale_quadrant(q):
            nc.sync.dma_start(
                vs_plane[32 * q : 32 * q + PACK, :].bitcast(I32), vs_scales[0, PACK * q : PACK * (q + 1), :].bitcast(I32)
            )

        xo_staged = sb("xo_staged", [PACK, QUADS, Z // 4], I32)
        load_scale_rows(xo_staged, 0, xo_scales)
        step = sb("step", [P, PACK], F32)
        nc.sync.dma_start(step[:], gs.rearrange("(p t) o -> p (t o)", t=PACK))
        idx = load_list("idx", offs)
        cq_rows = cq.rearrange("(p t) c -> t p c", t=PACK)
        cq_sb = [sb("cq%d" % t, [P, T], F32) for t in range(PACK - 1)] + [placed("cq3", [P, T], F32, 0)]
        nc.sync.dma_start(cq_sb[0][:], cq_rows[0])
        load_scale_rows(ww_staged, 68, w_scales)
        load_scale_rows(ww_staged, 64, w2_scales)
        nc.sync.dma_start(cq_sb[1][:], cq_rows[1])
        idx2 = load_list("idx2", offs2)
        nc.sync.dma_start(cq_sb[2][:], cq_rows[2])
        idx7 = load_list("idx7", offs7)
        for q in range(QUADS - 1):
            load_vs_scale_quadrant(q)
        nc.sync.dma_start(cq_sb[3][:], cq_rows[3])
        load_vs_scale_quadrant(QUADS - 1)
        w_raw = placed("w_raw", [P, R], U32, 4096)
        nc.sync.dma_start(w_raw[:].bitcast(I32), w_words[0].rearrange("p c r -> p (c r)").bitcast(I32))
        w2_raw = sb("w2_raw", [P, R], U16)
        nc.sync.dma_start(w2_raw[:].bitcast(I32), w2_words[0].bitcast(I32))
        xo_all = placed("xo_all", [P, Z], U32, 16384)
        nc.sync.dma_start(xo_all[:].bitcast(I32), xo_words[0].rearrange("p c r -> p (c r)").bitcast(I32))
        idx3 = load_list("idx3", offs3)
        idx4 = load_list("idx4", offs4)
        idx6 = load_list("idx6", offs6)
        idx5 = load_list("idx5", offs5)
        vs_all = sb("vs_all", [P, S], U16)
        nc.sync.dma_start(vs_all[:].bitcast(I32), vs_words[0].bitcast(I32))

        spread_scale_rows([(xo_plane, xo_staged)], 0, PACK)
        ww_plane = sb("ww_plane", [P, R], U8)
        spread_scale_rows([(ww_plane, ww_staged)], 64, 32)
        ww_sc = sb("ww_sc", [P, R], U8)
        deal(nc.vector.tensor_copy, ww_sc, ww_plane)
        xo_sc = sb("xo_sc", [P, J], U8)
        nc.vector.tensor_copy(xo_sc[:], xo_plane[:].indirect(idx2[:]))
        vs_sc = sb("vs_sc", [P, N], U8)
        nc.vector.tensor_copy(vs_sc[:], vs_plane[:].indirect(idx7[:]))

        x1_planes = sb("x1_planes", [P, PACK, J], BF16)
        for t in range(PACK):
            nc.scalar.activation(x1_planes[:, t, :], cq_sb[t][:].indirect(idx[:]), COPY, scale=step[:, t : t + 1])
        w_dealt = placed("w_dealt", [P, R], U32, 0)
        deal(nc.scalar.copy, w_dealt, w_raw)
        w2_dealt = placed("w2_dealt", [P, R], U16, 4096)
        deal(nc.scalar.copy, w2_dealt, w2_raw)
        x1_woven = placed("x1_woven", [P, J, PACK], BF16, 8192)
        halves = [slice(0, J // 2), slice(J // 2, J)]
        for js in halves:
            nc.vector.tensor_copy(
                x1_woven[:, js, :].rearrange("p (c i) t -> p c t i", i=4),
                x1_planes[:, :, js].rearrange("p t (c i) -> p c t i", i=4),
            )
        x1_codes = sb("x1_codes", [P, J], U32)
        x1_sc = sb("x1_sc", [P, J], U8)
        for js in halves:
            nc.vector.quantize_mx(
                x1_codes[:, js].bitcast(E4M3X4), x1_sc[:, js], x1_woven[:, js, :].rearrange("p j t -> p (j t)")
            )
        xo_g = placed("xo_g", [P, J], U32, 8192)
        nc.vector.tensor_copy(xo_g[:], xo_all[:].indirect(idx2[:]))

        a_acc = [psum.tile([P, J], F32, name="a_acc%d" % t, tag="bank_a%d" % t) for t in range(PACK)]
        for t in range(PACK):
            nc.tensor.matmul_mx(
                a_acc[t][:],
                lhsT=w_dealt[:, t * P : (t + 1) * P].bitcast(E4M3X4),
                lhsT_scale=ww_sc[4:P, t * P : (t + 1) * P],
                rhs=x1_codes[:].bitcast(E4M3X4),
                rhs_scale=x1_sc[:],
                start=True,
                stop=True,
            )
        b_acc = [psum.tile([P, J], F32, name="b_acc%d" % t, tag="bank_b%d" % t) for t in range(PACK)]
        for t in range(PACK):
            nc.tensor.matmul_mx(
                b_acc[t][:],
                lhsT=w2_dealt[:, t * P : (t + 1) * P].bitcast(E2M1X4),
                lhsT_scale=ww_sc[:, t * P : (t + 1) * P],
                rhs=xo_g[:].bitcast(E4M3X4),
                rhs_scale=xo_sc[:],
                start=True,
                stop=True,
            )

        a_sb = [sb("a%d" % t, [P, J], F32) for t in range(PACK - 1)] + [placed("a3", [P, J], F32, 16384)]
        b_sb = [sb("b%d" % t, [P, J], F32) for t in range(PACK)]
        for t in range(3):
            nc.scalar.copy(a_sb[t][:], a_acc[t][:])
        nc.vector.tensor_copy(pw[0][:].indirect(idx3[:]), a_sb[0][:])
        nc.vector.tensor_copy(a_sb[3][:], a_acc[3][:])
        nc.scalar.activation(pw[1][:].indirect(idx3[:]), a_sb[1][:], COPY)
        nc.vector.tensor_copy(pw[2][:].indirect(idx3[:]), a_sb[2][:])
        nc.vector.tensor_copy(pw[3][:].indirect(idx3[:]), a_sb[3][:])
        for t in range(2):
            nc.scalar.copy(b_sb[t][:], b_acc[t][:])
        for t in range(2, PACK):
            nc.vector.tensor_copy(b_sb[t][:], b_acc[t][:])

        diff = sb("diff", [P, PACK, O], F32)
        rival = [sb("rival%d" % t, [P, C], F32) for t in range(PACK)]
        pg = [sb("pg%d" % t, [P, C], F32) for t in range(PACK)]
        b_led = [sb("b_led%d" % t, [P, O], F32) for t in range(PACK - 1)] + [placed("b_led3", [P, O], F32, 12288)]
        for pair in ((0, 1), (2, 3)):
            for t in pair:
                nc.scalar.activation(rival[t][:], pw[t][:].indirect(idx4[:]), COPY, scale=b_sb[t][:, 0:1])
                nc.vector.tensor_tensor(pg[t][:], pw[t][:, 0:C], rival[t][:], ALU.max)
            for t in pair:
                nc.scalar.activation(b_led[t][:], b_sb[t][:].indirect(idx6[:]), COPY, scale=a_sb[t][:, 0:1])
                nc.vector.tensor_tensor(diff[:, t, :], pg[t][:].indirect(idx5[:]), b_led[t][:], ALU.subtract)

        hid = sb("hid", [P, O, PACK], BF16)
        nc.scalar.activation(
            hid[:].rearrange("p (c i) t -> p c t i", i=4), diff[:].rearrange("p t (c i) -> p c t i", i=4), ABS
        )
        vs_g = placed("vs_g", [P, N], U16, 12288)
        nc.vector.tensor_copy(vs_g[:], vs_all[:].indirect(idx7[:]))
        hid_codes = sb("hid_codes", [P, O], U32)
        hid_sc = sb("hid_sc", [P, O], U8)
        nc.vector.quantize_mx(hid_codes[:].bitcast(E5M2X4), hid_sc[:], hid[:].rearrange("p o t -> p (o t)"))

        for h in range(N // P):
            acc = psum.tile([P, O], F32, name="y_acc%d" % h, tag="bank_a%d" % h)
            nc.tensor.matmul_mx(
                acc[:],
                lhsT=vs_g[:, h * P : (h + 1) * P].bitcast(E2M1X4),
                lhsT_scale=vs_sc[:, h * P : (h + 1) * P],
                rhs=hid_codes[:].bitcast(E5M2X4),
                rhs_scale=hid_sc[:],
                start=True,
                stop=True,
            )
            y = sb("y%d" % h, [P, O], F32)
            if h == 0:
                nc.vector.tensor_copy(y[:], acc[:])
                nc.sync.dma_start(out[0:P, :], y[:])
            else:
                nc.scalar.copy(y[:], acc[:])
                nc.scalar.dma_start(out[P : 2 * P, :], y[:])
